import numpy as np
import ml_dtypes


def mxq(x, axis, fmt="e4m3"):
    dtype, down = {"e4m3": (ml_dtypes.float8_e4m3fn, 7), "e5m2": (ml_dtypes.float8_e5m2, 14)}[fmt]
    v = np.moveaxis(np.asarray(x, np.float32).astype(ml_dtypes.bfloat16).astype(np.float64), axis, -1)
    blocks = v.reshape(v.shape[:-1] + (-1, 32))
    amax = np.abs(blocks).max(-1, keepdims=True)
    byte = np.maximum(np.where(amax > 0, np.frexp(amax)[1] - 1 + 127, 0) - down, 1)
    scale = np.exp2(byte - 127.0)
    codes = (blocks / scale).astype(np.float32).astype(dtype).astype(np.float64)
    return np.moveaxis((codes * scale).reshape(v.shape), -1, axis)


WIDE = False


def mx_kscale(k):
    if not WIDE:
        return np.ones(k)
    levels = np.array([10, -10, 5, -5, 0])
    if k % 512:
        return np.exp2(np.random.permutation(np.resize(levels, k // 32))).repeat(32)
    a = np.empty((k // 512, 16))
    for p in range(k // 512):
        a[p, :8] = np.random.permutation(np.resize(levels, 8))
        for g in range(8):
            far = levels[np.abs(levels - a[p, g]) >= 10]
            a[p, g + 8] = far[np.random.randint(len(far))]
    return np.exp2(a.ravel()).repeat(32)


def f64(x):
    return np.asarray(x).astype(np.float64)


def striped(idx):
    return np.tile(np.asarray(idx).reshape(-1, 16).T, (8, 1)).astype(np.uint16)


def unstriped(offs):
    return offs[:16].T.reshape(-1).astype(np.int64)


E2M1 = np.array([0.0, 0.5, 1.0, 1.5, 2.0, 3.0, 4.0, 6.0, -0.0, -0.5, -1.0, -1.5, -2.0, -3.0, -4.0, -6.0])


def pack_weight(w, fmt):
    k, n = w.shape
    w = f64(np.asarray(w, np.float32).astype(ml_dtypes.bfloat16)).reshape(k // 32, 32, n)
    amax = np.abs(w).max(1)
    if fmt == "e4m3":
        byte = np.frexp(amax)[1] - 1 + 127 - 7
    else:
        mant, ex = np.frexp(amax / 6.0)
        byte = np.where(mant > 0.5, ex, ex - 1) + 127
    byte = np.clip(np.where(amax > 0, byte, 1), 1, 254)
    scaled = (w * np.exp2(127.0 - byte)[:, None, :]).reshape(k, n).astype(np.float32)
    by_word = np.ascontiguousarray(scaled.reshape(k // 512, 128, 4, n).transpose(0, 1, 3, 2))
    if fmt == "e4m3":
        words = by_word.astype(ml_dtypes.float8_e4m3fn).view(np.uint8)
    else:
        c = by_word.astype(ml_dtypes.float4_e2m1fn).view(np.uint8) & 0xF
        words = (c[..., 0::2] | (c[..., 1::2] << 4)).reshape(k // 512, 128, 2 * n)
    return np.ascontiguousarray(words), np.ascontiguousarray(byte.astype(np.uint8).reshape(k // 512, 16, n))


def unpack_weight(words, scales, fmt):
    g, _, n = scales.shape
    words = np.ascontiguousarray(words).reshape(g, 128, n, -1)
    if fmt == "e4m3":
        vals = words.view(ml_dtypes.float8_e4m3fn).astype(np.float64)
    else:
        nib = np.empty((g, 128, n, 4), np.uint8)
        nib[..., 0::2] = words & 0xF
        nib[..., 1::2] = words >> 4
        vals = E2M1[nib]
    vals = vals * np.repeat(np.exp2(scales.astype(np.float64) - 127.0), 8, axis=1)[..., None]
    return vals.transpose(0, 1, 3, 2).reshape(g * 512, n)


def bf(x):
    return np.asarray(x, np.float32).astype(ml_dtypes.bfloat16)


def planes(Y):
    r, m = Y.shape
    b = f64(bf(Y)).reshape(r // 32, 32, m)
    amax = np.abs(b).max(1)
    byte = np.clip(np.where(amax > 0, np.frexp(amax)[1] - 1 + 127 - 7, 1), 1, 254)
    codes = (b * np.exp2(127.0 - byte)[:, None, :]).reshape(r, m).astype(np.float32).astype(ml_dtypes.float8_e4m3fn).view(np.uint8)
    words = codes.reshape(r // 512, 128, 4, m).transpose(0, 1, 3, 2)
    return np.ascontiguousarray(words), np.ascontiguousarray(byte.astype(np.uint8).reshape(r // 512, 16, m))


K, T, S, I, J, C, N = 1024, 1024, 1024, 512, 512, 1024, 512


def setup_inputs():
    n = np.random.standard_normal
    idx = np.random.permutation(T)[:I]
    idx2 = np.random.permutation(S)[:J]
    fk = mx_kscale(K)
    wp = pack_weight(n((K, N)) * 1 / np.sqrt(K) * fk[:, None], "e4m3")
    return {
        "xa": (n((K, T)) / fk[:, None]).astype(np.float32),
        "xb": (n((K, S)) * 0.5 / fk[:, None]).astype(np.float32),
        "w_words": wp[0],
        "w_scales": wp[1],
        "rw": (np.random.uniform(0.5, 2.0, (1, C))).astype(np.float32),
        "offs": striped(idx),
        "offs2": striped(idx2),
    }


def reference(xa, xb, w_words, w_scales, rw, offs, offs2):
    idx = unstriped(offs)
    idx2 = unstriped(offs2)
    wu = unpack_weight(w_words, w_scales, "e4m3")
    xc = np.concatenate([f64(xa)[:, idx], f64(xb)[:, idx2]], axis=1)
    xcq = mxq(xc, 0, "e4m3")
    z = wu.T @ xcq
    y = np.maximum(z, 0.0) * f64(rw)
    words, scales = planes(y)
    return y, words, scales

@@ -1,0 +1,174 @@
+from contextlib import ExitStack
+
+import concourse.mybir as mybir
+from concourse.masks import make_identity
+
+K, T, N, C = 1024, 1024, 512, 1024
+FLOPS = 2 * K * N * C
+
+F32 = mybir.dt.float32
+BF16 = mybir.dt.bfloat16
+I32 = mybir.dt.int32
+U32 = mybir.dt.uint32
+U16 = mybir.dt.uint16
+U8 = mybir.dt.uint8
+FP8X4 = mybir.dt.float8_e4m3fn_x4
+ALU = mybir.AluOpType
+
+P = 128
+PACK = 4
+PASSES = K // (P * PACK)
+HALF = C // 2
+CHUNK = 128
+CHUNKS = HALF // CHUNK
+LIST_COLS = HALF // 16
+
+
+def tile_list_two_tables_one_batch_pl_kernel(tc, xa, xb, w_words, w_scales, rw, offs, offs2, out_0, out_1, out_2):
+    nc = tc.nc
+    with ExitStack() as ctx:
+        keep = ctx.enter_context(tc.tile_pool(name="keep", bufs=1))
+        psum = ctx.enter_context(tc.psum_pool(name="psum", bufs=1))
+
+        def bank(i):
+            return psum.tile([P, 512], F32, name="bank%d" % i, tag="bank%d" % i)
+
+        lists = [keep.tile([P, LIST_COLS], U16, name="list%d" % i) for i in range(2)]
+        planes = {}
+
+        def load_plane(tbl, z, t):
+            src = (xa, xb)[tbl].rearrange("(z p t) c -> z t p c", z=PASSES, t=PACK)
+            tile = keep.tile([P, T], F32, name="plane%d%d%d" % (tbl, z, t))
+            nc.sync.dma_start(out=tile[:], in_=src[z, t])
+            planes[tbl, z, t] = tile
+
+        ws_raw = keep.tile([P, N], U8, align_bytes=64)
+        nc.vector.memset(ws_raw[:].bitcast(I32), 0)
+        nc.sync.dma_start(lists[0][:], offs)
+        load_plane(0, 0, 0)
+        w_raw = keep.tile([P, PASSES, N], U32, align_bytes=64)
+        nc.sync.dma_start(out=w_raw[:].bitcast(I32), in_=w_words.rearrange("z p n r -> p z (n r)").bitcast(I32))
+        for q in range(4):
+            nc.scalar.dma_start(
+                out=ws_raw[32 * q : 32 * q + 4 * PASSES, :].bitcast(I32),
+                in_=w_scales[:, 4 * q : 4 * q + 4, :].bitcast(I32),
+            )
+        for t in range(1, PACK):
+            load_plane(0, 0, t)
+        nc.sync.dma_start(lists[1][:], offs2)
+        for tbl, z in ((0, 1), (1, 0), (1, 1)):
+            for t in range(PACK):
+                load_plane(tbl, z, t)
+
+        ident = keep.tile([P, P], F32)
+        make_identity(nc, ident[:])
+        rw_col = keep.tile([P, 8], F32)
+        nc.gpsimd.dma_start(out=rw_col[:], in_=rw[0].rearrange("(n j) -> n j", j=8))
+        rw_all = keep.tile([P, C], F32)
+        for h in range(2):
+            spread = bank(4 + h)
+            for j in range(4):
+                col = 4 * h + j
+                nc.tensor.transpose(spread[:, P * j : P * (j + 1)], rw_col[:, col : col + 1].to_broadcast([P, P]), ident[:])
+            nc.scalar.copy(
+                out=rw_all[:].rearrange("p (n j) -> p n j", j=8)[:, :, 4 * h : 4 * h + 4],
+                in_=spread[:].rearrange("p (j n) -> p n j", j=4),
+            )
+
+        w_codes = keep.tile([P, PASSES, PACK, P], U32, align_bytes=64)
+        w_sc = keep.tile([P, PACK, P], U8, align_bytes=64)
+
+        def deal_weights():
+            nc.vector.tensor_copy(out=w_codes[:], in_=w_raw[:].rearrange("p z (m t) -> p z t m", t=PACK))
+            nc.vector.tensor_copy(out=w_sc[:], in_=ws_raw[:].rearrange("p (m t) -> p t m", t=PACK))
+
+        def gather(picked, tbl, z, t, c0, c1):
+            nc.vector.tensor_copy(picked[:, t, c0:c1], planes[tbl, z, t][:].indirect(lists[tbl][:, c0 // 16 : c1 // 16]))
+
+        def interleave(name, rows, width):
+            grouped = keep.tile([P, width * PACK], BF16, name=name, align_bytes=64)
+            nc.scalar.copy(
+                out=grouped[:].rearrange("p (c i t) -> p c t i", i=4, t=PACK),
+                in_=rows.rearrange("p t (c i) -> p c t i", i=4),
+            )
+            return grouped
+
+        def quantise_x(name, grouped, width):
+            codes = keep.tile([P, width], U32, name=name + "c", align_bytes=64)
+            scales = keep.tile([P, width], U8, name=name + "s", align_bytes=64)
+            nc.vector.quantize_mx(out=codes[:].bitcast(FP8X4), scales=scales[:], in_=grouped[:])
+            return codes, scales
+
+        def product(acc, z, t, codes, scales, start, stop):
+            nc.tensor.matmul_mx(
+                out=acc,
+                lhsT=w_codes[:, z, t, :].bitcast(FP8X4),
+                lhsT_scale=w_sc[4 * z : P, t, :],
+                rhs=codes.bitcast(FP8X4),
+                rhs_scale=scales,
+                start=start,
+                stop=stop,
+            )
+
+        out_rows = out_0.rearrange("(p t) c -> p t c", t=PACK)
+        out_words = out_1[0].rearrange("p c r -> p (c r)")
+        y_scales = keep.tile([P, C], U8, align_bytes=64)
+
+        def hand_on(name, y, c0, width):
+            grouped = interleave(name + "g", y[:], width)
+            codes = keep.tile([P, width], U32, name=name + "c", align_bytes=64)
+            nc.vector.quantize_mx(out=codes[:].bitcast(FP8X4), scales=y_scales[:, c0 : c0 + width], in_=grouped[:])
+            nc.sync.dma_start(out=out_words[:, PACK * c0 : PACK * (c0 + width)].bitcast(I32), in_=codes[:].bitcast(I32))
+
+        def whole_pass(tbl, z):
+            picked = keep.tile([P, PACK, HALF], F32, name="picked%d%d" % (tbl, z))
+            for t in range(PACK):
+                gather(picked, tbl, z, t, 0, HALF)
+                if (tbl, z, t) == (0, 0, 0):
+                    deal_weights()
+            name = "x%d%d" % (tbl, z)
+            return quantise_x(name, interleave(name + "g", picked[:], HALF), HALF)
+
+        acc_a = [bank(t) for t in range(PACK)]
+        for z in range(PASSES):
+            codes, scales = whole_pass(0, z)
+            for t in range(PACK):
+                product(acc_a[t][:], z, t, codes[:], scales[:], z == 0, z == PASSES - 1)
+        y_a = keep.tile([P, PACK, HALF], F32)
+        for t in range(PACK):
+            nc.vector.scalar_tensor_tensor(y_a[:, t, :], acc_a[t][:], 0.0, rw_all[:, 0:HALF], ALU.max, ALU.mult)
+            nc.sync.dma_start(out=out_rows[:, t, 0:HALF], in_=y_a[:, t, :])
+        hand_on("ya", y_a, 0, HALF)
+
+        acc_b = [bank(4 + j) for j in range(CHUNKS)]
+        codes, scales = whole_pass(1, 0)
+        for j in range(CHUNKS):
+            cols = slice(CHUNK * j, CHUNK * (j + 1))
+            for t in range(PACK):
+                product(acc_b[j][:, CHUNK * t : CHUNK * (t + 1)], 0, t, codes[:, cols], scales[:, cols], t == 0, False)
+        picked = keep.tile([P, PACK, HALF], F32, name="picked11")
+        for t in range(PACK - 1):
+            gather(picked, 1, 1, t, 0, HALF)
+        for j in range(CHUNKS):
+            gather(picked, 1, 1, PACK - 1, CHUNK * j, CHUNK * (j + 1))
+        for j in range(CHUNKS):
+            c0 = HALF + CHUNK * j
+            name = "x11%d" % j
+            codes, scales = quantise_x(name, interleave(name + "g", picked[:, :, CHUNK * j : CHUNK * (j + 1)], CHUNK), CHUNK)
+            for t in range(PACK):
+                product(acc_b[j][:, CHUNK * t : CHUNK * (t + 1)], 1, t, codes[:], scales[:], False, t == PACK - 1)
+            y_b = keep.tile([P, PACK, CHUNK], F32, name="yb%d" % j)
+            nc.vector.scalar_tensor_tensor(
+                y_b[:],
+                acc_b[j][:].rearrange("p (t c) -> p t c", t=PACK),
+                0.0,
+                rw_all[:, c0 : c0 + CHUNK].unsqueeze(1).to_broadcast([P, PACK, CHUNK]),
+                ALU.max,
+                ALU.mult,
+            )
+            nc.sync.dma_start(out=out_rows[:, :, c0 : c0 + CHUNK], in_=y_b[:])
+            hand_on("yb%d" % j, y_b, c0, CHUNK)
+
+        for q in range(4):
+            queue = nc.scalar if q % 2 else nc.sync
+            queue.dma_start(out=out_2[0, 4 * q : 4 * q + 4, :].bitcast(I32), in_=y_scales[32 * q : 32 * q + 4, :].bitcast(I32))

@@ -38,32 +38,41 @@ def tile_list_two_tables_one_batch_pl_kernel(tc, xa, xb, w_words, w_scales, rw, 
 
         def load_plane(tbl, z, t):
             src = (xa, xb)[tbl].rearrange("(z p t) c -> z t p c", z=PASSES, t=PACK)
-            tile = keep.tile([P, T], F32, name="plane%d%d%d" % (tbl, z, t))
+            name = "plane%d%d%d" % (tbl, z, t)
+            tile = keep.tile([P, T], F32, name=name, tag=name, align_bytes=64)
             nc.sync.dma_start(out=tile[:], in_=src[z, t])
             planes[tbl, z, t] = tile
 
         ws_raw = keep.tile([P, N], U8, align_bytes=64)
         nc.vector.memset(ws_raw[:].bitcast(I32), 0)
+        w_raw = [keep.tile([P, N], U32, name="w_raw%d" % z, align_bytes=64) for z in range(PASSES)]
+
+        def load_words(z):
+            nc.sync.dma_start(out=w_raw[z][:].bitcast(I32), in_=w_words[z].rearrange("p n r -> p (n r)").bitcast(I32))
+
         nc.sync.dma_start(lists[0][:], offs)
-        load_plane(0, 0, 0)
-        w_raw = keep.tile([P, PASSES, N], U32, align_bytes=64)
-        nc.sync.dma_start(out=w_raw[:].bitcast(I32), in_=w_words.rearrange("z p n r -> p z (n r)").bitcast(I32))
         for q in range(4):
             nc.scalar.dma_start(
                 out=ws_raw[32 * q : 32 * q + 4 * PASSES, :].bitcast(I32),
                 in_=w_scales[:, 4 * q : 4 * q + 4, :].bitcast(I32),
             )
-        for t in range(1, PACK):
+        for t in range(PACK):
             load_plane(0, 0, t)
+        load_words(0)
+        load_plane(0, 1, 0)
+        load_plane(0, 1, 1)
+        load_words(1)
+        load_plane(0, 1, 2)
+        load_plane(0, 1, 3)
         nc.sync.dma_start(lists[1][:], offs2)
-        for tbl, z in ((0, 1), (1, 0), (1, 1)):
+        for z in range(PASSES):
             for t in range(PACK):
-                load_plane(tbl, z, t)
+                load_plane(1, z, t)
 
         ident = keep.tile([P, P], F32)
         make_identity(nc, ident[:])
         rw_col = keep.tile([P, 8], F32)
-        nc.gpsimd.dma_start(out=rw_col[:], in_=rw[0].rearrange("(n j) -> n j", j=8))
+        nc.scalar.dma_start(out=rw_col[:], in_=rw[0].rearrange("(n j) -> n j", j=8))
         rw_all = keep.tile([P, C], F32)
         for h in range(2):
             spread = bank(4 + h)
@@ -78,15 +87,17 @@ def tile_list_two_tables_one_batch_pl_kernel(tc, xa, xb, w_words, w_scales, rw, 
         w_codes = keep.tile([P, PASSES, PACK, P], U32, align_bytes=64)
         w_sc = keep.tile([P, PACK, P], U8, align_bytes=64)
 
-        def deal_weights():
-            nc.vector.tensor_copy(out=w_codes[:], in_=w_raw[:].rearrange("p z (m t) -> p z t m", t=PACK))
-            nc.vector.tensor_copy(out=w_sc[:], in_=ws_raw[:].rearrange("p (m t) -> p t m", t=PACK))
+        for t in range(PACK):
+            nc.gpsimd.tensor_copy(out=w_sc[:, t, :], in_=ws_raw[:].rearrange("p (m t) -> p t m", t=PACK)[:, t, :])
+        for z in range(PASSES):
+            for t in range(PACK):
+                nc.gpsimd.tensor_copy(out=w_codes[:, z, t, :], in_=w_raw[z][:].rearrange("p (m t) -> p t m", t=PACK)[:, t, :])
 
         def gather(picked, tbl, z, t, c0, c1):
             nc.vector.tensor_copy(picked[:, t, c0:c1], planes[tbl, z, t][:].indirect(lists[tbl][:, c0 // 16 : c1 // 16]))
 
-        def interleave(name, rows, width):
-            grouped = keep.tile([P, width * PACK], BF16, name=name, align_bytes=64)
+        def interleave(name, rows, width, tag=None):
+            grouped = keep.tile([P, width * PACK], BF16, name=name, tag=tag or name, align_bytes=64)
             nc.scalar.copy(
                 out=grouped[:].rearrange("p (c i t) -> p c t i", i=4, t=PACK),
                 in_=rows.rearrange("p t (c i) -> p c t i", i=4),
@@ -114,53 +125,76 @@ def tile_list_two_tables_one_batch_pl_kernel(tc, xa, xb, w_words, w_scales, rw, 
         out_words = out_1[0].rearrange("p c r -> p (c r)")
         y_scales = keep.tile([P, C], U8, align_bytes=64)
 
-        def hand_on(name, y, c0, width):
-            grouped = interleave(name + "g", y[:], width)
+        def hand_on(name, y, c0, width, tag=None):
+            grouped = interleave(name + "g", y[:], width, tag)
             codes = keep.tile([P, width], U32, name=name + "c", align_bytes=64)
             nc.vector.quantize_mx(out=codes[:].bitcast(FP8X4), scales=y_scales[:, c0 : c0 + width], in_=grouped[:])
             nc.sync.dma_start(out=out_words[:, PACK * c0 : PACK * (c0 + width)].bitcast(I32), in_=codes[:].bitcast(I32))
 
-        def whole_pass(tbl, z):
-            picked = keep.tile([P, PACK, HALF], F32, name="picked%d%d" % (tbl, z))
+        def first_pass(tbl, acc, width):
+            picked = keep.tile([P, PACK, HALF], F32, name="picked%d0" % tbl)
             for t in range(PACK):
-                gather(picked, tbl, z, t, 0, HALF)
-                if (tbl, z, t) == (0, 0, 0):
-                    deal_weights()
-            name = "x%d%d" % (tbl, z)
-            return quantise_x(name, interleave(name + "g", picked[:], HALF), HALF)
+                gather(picked, tbl, 0, t, 0, HALF)
+            name = "x%d0" % tbl
+            codes, scales = quantise_x(name, interleave(name + "g", picked[:], HALF), HALF)
+            per_bank = 512 // width
+            for j in range(HALF // width):
+                cols = slice(width * j, width * (j + 1))
+                for t in range(PACK):
+                    product(acc(j, t), 0, t, codes[:, cols], scales[:, cols], t % per_bank == 0, False)
 
-        acc_a = [bank(t) for t in range(PACK)]
-        for z in range(PASSES):
-            codes, scales = whole_pass(0, z)
+        def second_pass(tbl, picked, acc, j, width):
+            name = "x%d1_%d" % (tbl, j)
+            cols = slice(width * j, width * (j + 1))
+            codes, scales = quantise_x(name, interleave(name + "g", picked[:, :, cols], width), width)
+            per_bank = 512 // width
             for t in range(PACK):
-                product(acc_a[t][:], z, t, codes[:], scales[:], z == 0, z == PASSES - 1)
-        y_a = keep.tile([P, PACK, HALF], F32)
+                product(acc(j, t), 1, t, codes[:], scales[:], False, t % per_bank == per_bank - 1)
+
+        WA = 256
+        banks_a = [bank(i) for i in range(4)]
+
+        def acc_a(j, t):
+            return banks_a[2 * j + t // 2][:, WA * (t % 2) : WA * (t % 2 + 1)]
+
+        first_pass(0, acc_a, WA)
+        picked = keep.tile([P, PACK, HALF], F32, name="picked01")
         for t in range(PACK):
-            nc.vector.scalar_tensor_tensor(y_a[:, t, :], acc_a[t][:], 0.0, rw_all[:, 0:HALF], ALU.max, ALU.mult)
-            nc.sync.dma_start(out=out_rows[:, t, 0:HALF], in_=y_a[:, t, :])
-        hand_on("ya", y_a, 0, HALF)
+            gather(picked, 0, 1, t, 0, HALF)
+        for j in range(HALF // WA):
+            second_pass(0, picked, acc_a, j, WA)
+        ys_a = []
+        for j in range(HALF // WA):
+            c0 = WA * j
+            y_a = keep.tile([P, PACK, WA], F32, name="ya%d" % j)
+            for h in range(2):
+                kept = keep.tile([P, 2, WA], F32, name="kept%d%d" % (j, h))
+                nc.scalar.activation(kept[:].rearrange("p t c -> p (t c)"), banks_a[2 * j + h][:], mybir.ActivationFunctionType.Relu)
+                for u in range(2):
+                    nc.gpsimd.tensor_tensor(y_a[:, 2 * h + u, :], kept[:, u, :], rw_all[:, c0 : c0 + WA], ALU.mult)
+            nc.sync.dma_start(out=out_rows[:, :, c0 : c0 + WA], in_=y_a[:])
+            ys_a.append(y_a)
 
-        acc_b = [bank(4 + j) for j in range(CHUNKS)]
-        codes, scales = whole_pass(1, 0)
-        for j in range(CHUNKS):
-            cols = slice(CHUNK * j, CHUNK * (j + 1))
-            for t in range(PACK):
-                product(acc_b[j][:, CHUNK * t : CHUNK * (t + 1)], 0, t, codes[:, cols], scales[:, cols], t == 0, False)
+        banks_b = [bank(4 + j) for j in range(CHUNKS)]
+
+        def acc_b(j, t):
+            return banks_b[j][:, CHUNK * t : CHUNK * (t + 1)]
+
+        first_pass(1, acc_b, CHUNK)
         picked = keep.tile([P, PACK, HALF], F32, name="picked11")
         for t in range(PACK - 1):
             gather(picked, 1, 1, t, 0, HALF)
+            if t < len(ys_a):
+                hand_on("ya%d" % t, ys_a[t], WA * t, WA, "plane11%d" % t)
         for j in range(CHUNKS):
             gather(picked, 1, 1, PACK - 1, CHUNK * j, CHUNK * (j + 1))
         for j in range(CHUNKS):
             c0 = HALF + CHUNK * j
-            name = "x11%d" % j
-            codes, scales = quantise_x(name, interleave(name + "g", picked[:, :, CHUNK * j : CHUNK * (j + 1)], CHUNK), CHUNK)
-            for t in range(PACK):
-                product(acc_b[j][:, CHUNK * t : CHUNK * (t + 1)], 1, t, codes[:], scales[:], False, t == PACK - 1)
+            second_pass(1, picked, acc_b, j, CHUNK)
             y_b = keep.tile([P, PACK, CHUNK], F32, name="yb%d" % j)
             nc.vector.scalar_tensor_tensor(
                 y_b[:],
-                acc_b[j][:].rearrange("p (t c) -> p t c", t=PACK),
+                banks_b[j][:].rearrange("p (t c) -> p t c", t=PACK),
                 0.0,
                 rw_all[:, c0 : c0 + CHUNK].unsqueeze(1).to_broadcast([P, PACK, CHUNK]),
                 ALU.max,

from contextlib import ExitStack

import concourse.mybir as mybir
from concourse.masks import make_identity

K, T, N, C = 1024, 1024, 512, 1024
FLOPS = 2 * K * N * C

F32 = mybir.dt.float32
BF16 = mybir.dt.bfloat16
I32 = mybir.dt.int32
U32 = mybir.dt.uint32
U16 = mybir.dt.uint16
U8 = mybir.dt.uint8
FP8X4 = mybir.dt.float8_e4m3fn_x4
ALU = mybir.AluOpType

P = 128
PACK = 4
PASSES = K // (P * PACK)
HALF = C // 2
CHUNK = 128
CHUNKS = HALF // CHUNK
LIST_COLS = HALF // 16


def tile_list_two_tables_one_batch_pl_kernel(tc, xa, xb, w_words, w_scales, rw, offs, offs2, out_0, out_1, out_2):
    nc = tc.nc
    with ExitStack() as ctx:
        keep = ctx.enter_context(tc.tile_pool(name="keep", bufs=1))
        psum = ctx.enter_context(tc.psum_pool(name="psum", bufs=1))

        def bank(i):
            return psum.tile([P, 512], F32, name="bank%d" % i, tag="bank%d" % i)

        lists = [keep.tile([P, LIST_COLS], U16, name="list%d" % i) for i in range(2)]
        planes = {}

        def load_plane(tbl, z, t):
            src = (xa, xb)[tbl].rearrange("(z p t) c -> z t p c", z=PASSES, t=PACK)
            name = "plane%d%d%d" % (tbl, z, t)
            tile = keep.tile([P, T], F32, name=name, tag=name, align_bytes=64)
            nc.sync.dma_start(out=tile[:], in_=src[z, t])
            planes[tbl, z, t] = tile

        ws_raw = keep.tile([P, N], U8, align_bytes=64)
        nc.vector.memset(ws_raw[:].bitcast(I32), 0)
        w_raw = [keep.tile([P, N], U32, name="w_raw%d" % z, align_bytes=64) for z in range(PASSES)]

        def load_words(z):
            nc.sync.dma_start(out=w_raw[z][:].bitcast(I32), in_=w_words[z].rearrange("p n r -> p (n r)").bitcast(I32))

        nc.sync.dma_start(lists[0][:], offs)
        for q in range(4):
            nc.scalar.dma_start(
                out=ws_raw[32 * q : 32 * q + 4 * PASSES, :].bitcast(I32),
                in_=w_scales[:, 4 * q : 4 * q + 4, :].bitcast(I32),
            )
        for t in range(PACK):
            load_plane(0, 0, t)
        load_words(0)
        load_plane(0, 1, 0)
        load_plane(0, 1, 1)
        load_words(1)
        load_plane(0, 1, 2)
        load_plane(0, 1, 3)
        nc.sync.dma_start(lists[1][:], offs2)
        for z in range(PASSES):
            for t in range(PACK):
                load_plane(1, z, t)

        ident = keep.tile([P, P], F32)
        make_identity(nc, ident[:])
        rw_col = keep.tile([P, 8], F32)
        nc.scalar.dma_start(out=rw_col[:], in_=rw[0].rearrange("(n j) -> n j", j=8))
        rw_all = keep.tile([P, C], F32)
        for h in range(2):
            spread = bank(4 + h)
            for j in range(4):
                col = 4 * h + j
                nc.tensor.transpose(spread[:, P * j : P * (j + 1)], rw_col[:, col : col + 1].to_broadcast([P, P]), ident[:])
            nc.scalar.copy(
                out=rw_all[:].rearrange("p (n j) -> p n j", j=8)[:, :, 4 * h : 4 * h + 4],
                in_=spread[:].rearrange("p (j n) -> p n j", j=4),
            )

        w_codes = keep.tile([P, PASSES, PACK, P], U32, align_bytes=64)
        w_sc = keep.tile([P, PACK, P], U8, align_bytes=64)

        for t in range(PACK):
            nc.gpsimd.tensor_copy(out=w_sc[:, t, :], in_=ws_raw[:].rearrange("p (m t) -> p t m", t=PACK)[:, t, :])
        for z in range(PASSES):
            for t in range(PACK):
                nc.gpsimd.tensor_copy(out=w_codes[:, z, t, :], in_=w_raw[z][:].rearrange("p (m t) -> p t m", t=PACK)[:, t, :])

        def gather(picked, tbl, z, t, c0, c1):
            nc.vector.tensor_copy(picked[:, t, c0:c1], planes[tbl, z, t][:].indirect(lists[tbl][:, c0 // 16 : c1 // 16]))

        def interleave(name, rows, width, tag=None):
            grouped = keep.tile([P, width * PACK], BF16, name=name, tag=tag or name, align_bytes=64)
            nc.scalar.copy(
                out=grouped[:].rearrange("p (c i t) -> p c t i", i=4, t=PACK),
                in_=rows.rearrange("p t (c i) -> p c t i", i=4),
            )
            return grouped

        def quantise_x(name, grouped, width):
            codes = keep.tile([P, width], U32, name=name + "c", align_bytes=64)
            scales = keep.tile([P, width], U8, name=name + "s", align_bytes=64)
            nc.vector.quantize_mx(out=codes[:].bitcast(FP8X4), scales=scales[:], in_=grouped[:])
            return codes, scales

        def product(acc, z, t, codes, scales, start, stop):
            nc.tensor.matmul_mx(
                out=acc,
                lhsT=w_codes[:, z, t, :].bitcast(FP8X4),
                lhsT_scale=w_sc[4 * z : P, t, :],
                rhs=codes.bitcast(FP8X4),
                rhs_scale=scales,
                start=start,
                stop=stop,
            )

        out_rows = out_0.rearrange("(p t) c -> p t c", t=PACK)
        out_words = out_1[0].rearrange("p c r -> p (c r)")
        y_scales = keep.tile([P, C], U8, align_bytes=64)

        def hand_on(name, y, c0, width, tag=None):
            grouped = interleave(name + "g", y[:], width, tag)
            codes = keep.tile([P, width], U32, name=name + "c", align_bytes=64)
            nc.vector.quantize_mx(out=codes[:].bitcast(FP8X4), scales=y_scales[:, c0 : c0 + width], in_=grouped[:])
            nc.sync.dma_start(out=out_words[:, PACK * c0 : PACK * (c0 + width)].bitcast(I32), in_=codes[:].bitcast(I32))

        def first_pass(tbl, acc, width):
            picked = keep.tile([P, PACK, HALF], F32, name="picked%d0" % tbl)
            for t in range(PACK):
                gather(picked, tbl, 0, t, 0, HALF)
            name = "x%d0" % tbl
            codes, scales = quantise_x(name, interleave(name + "g", picked[:], HALF), HALF)
            per_bank = 512 // width
            for j in range(HALF // width):
                cols = slice(width * j, width * (j + 1))
                for t in range(PACK):
                    product(acc(j, t), 0, t, codes[:, cols], scales[:, cols], t % per_bank == 0, False)

        def second_pass(tbl, picked, acc, j, width):
            name = "x%d1_%d" % (tbl, j)
            cols = slice(width * j, width * (j + 1))
            codes, scales = quantise_x(name, interleave(name + "g", picked[:, :, cols], width), width)
            per_bank = 512 // width
            for t in range(PACK):
                product(acc(j, t), 1, t, codes[:], scales[:], False, t % per_bank == per_bank - 1)

        WA = 256
        banks_a = [bank(i) for i in range(4)]

        def acc_a(j, t):
            return banks_a[2 * j + t // 2][:, WA * (t % 2) : WA * (t % 2 + 1)]

        first_pass(0, acc_a, WA)
        picked = keep.tile([P, PACK, HALF], F32, name="picked01")
        for t in range(PACK):
            gather(picked, 0, 1, t, 0, HALF)
        for j in range(HALF // WA):
            second_pass(0, picked, acc_a, j, WA)
        ys_a = []
        for j in range(HALF // WA):
            c0 = WA * j
            y_a = keep.tile([P, PACK, WA], F32, name="ya%d" % j)
            for h in range(2):
                kept = keep.tile([P, 2, WA], F32, name="kept%d%d" % (j, h))
                nc.scalar.activation(kept[:].rearrange("p t c -> p (t c)"), banks_a[2 * j + h][:], mybir.ActivationFunctionType.Relu)
                for u in range(2):
                    nc.gpsimd.tensor_tensor(y_a[:, 2 * h + u, :], kept[:, u, :], rw_all[:, c0 : c0 + WA], ALU.mult)
            nc.sync.dma_start(out=out_rows[:, :, c0 : c0 + WA], in_=y_a[:])
            ys_a.append(y_a)

        banks_b = [bank(4 + j) for j in range(CHUNKS)]

        def acc_b(j, t):
            return banks_b[j][:, CHUNK * t : CHUNK * (t + 1)]

        first_pass(1, acc_b, CHUNK)
        picked = keep.tile([P, PACK, HALF], F32, name="picked11")
        for t in range(PACK - 1):
            gather(picked, 1, 1, t, 0, HALF)
            if t < len(ys_a):
                hand_on("ya%d" % t, ys_a[t], WA * t, WA, "plane11%d" % t)
        for j in range(CHUNKS):
            gather(picked, 1, 1, PACK - 1, CHUNK * j, CHUNK * (j + 1))
        for j in range(CHUNKS):
            c0 = HALF + CHUNK * j
            second_pass(1, picked, acc_b, j, CHUNK)
            y_b = keep.tile([P, PACK, CHUNK], F32, name="yb%d" % j)
            nc.vector.scalar_tensor_tensor(
                y_b[:],
                banks_b[j][:].rearrange("p (t c) -> p t c", t=PACK),
                0.0,
                rw_all[:, c0 : c0 + CHUNK].unsqueeze(1).to_broadcast([P, PACK, CHUNK]),
                ALU.max,
                ALU.mult,
            )
            nc.sync.dma_start(out=out_rows[:, :, c0 : c0 + CHUNK], in_=y_b[:])
            hand_on("yb%d" % j, y_b, c0, CHUNK)

        for q in range(4):
            queue = nc.scalar if q % 2 else nc.sync
            queue.dma_start(out=out_2[0, 4 * q : 4 * q + 4, :].bitcast(I32), in_=y_scales[32 * q : 32 * q + 4, :].bitcast(I32))
